import numpy as np
import ml_dtypes

BF16 = ml_dtypes.bfloat16


def bf(x):
    return np.asarray(x, np.float32).astype(BF16)


def f32(x):
    return np.asarray(x, np.float32)


def f64(x):
    return np.asarray(x).astype(np.float64)


def striped(idx):
    return np.tile(idx.reshape(-1, 16).T, (8, 1))


S, K, M, N, E, Q, V, D = 256, 128, 512, 128, 1, 128, 32, 8


def setup_inputs():
    return {"base": bf(np.random.standard_normal((M, S))), "x": bf(np.random.standard_normal((K, N))), "w": bf(1.5 * np.random.standard_normal((E, K, M)) / np.sqrt(K)), "b": f32(0.5 * np.random.standard_normal((M, 1))), "offs": striped(np.random.permutation(S)[:N])}


def reference(base, x, w, b, offs):
    idx = offs[:16].T.reshape(-1)
    z = f64(base).copy()
    for e in range(E):
        z[:, idx[e * Q : (e + 1) * Q]] += f64(w)[e].T @ f64(x)[:, e * Q : (e + 1) * Q]
    z = np.tanh(z + f64(b))
    return z.reshape(M, V, D).mean(axis=2)

@@ -1,0 +1,56 @@
+import concourse.mybir as mybir
+from concourse.masks import make_identity
+
+P = 128
+D = 8
+
+BF16, F32, U16 = mybir.dt.bfloat16, mybir.dt.float32, mybir.dt.uint16
+FLOPS = 2 * 128 * 512 * 128
+
+
+def tile_rows_unpool_mean_tanh_kernel(tc, base, x, w, b, offs, out):
+    nc = tc.nc
+    M, S = base.shape
+    N = x.shape[1]
+    V = S // D
+    blocks = M // P
+
+    with (
+        tc.tile_pool(name="held", bufs=1) as held,
+        tc.psum_pool(name="windows", bufs=1) as windows,
+    ):
+        base_tile = held.tile([P, blocks, S], BF16)
+        nc.sync.dma_start(base_tile[:], base.rearrange("(a p) s -> p a s", p=P))
+        w_tile = held.tile([P, M], BF16)
+        nc.sync.dma_start(w_tile[:], w.rearrange("e k m -> k (e m)"))
+        x_tile = held.tile([P, N], BF16)
+        nc.sync.dma_start(x_tile[:], x)
+        offsets = held.tile([P, N // 16], U16)
+        nc.sync.dma_start(offsets[:], offs)
+        bias = held.tile([P, blocks], F32)
+        nc.scalar.dma_start(bias[:], b.rearrange("(a p) o -> p (a o)", p=P))
+
+        identity = held.tile([P, P], BF16)
+        make_identity(nc, identity[:])
+
+        window = [windows.tile([P, S], F32, name=f"window{a}") for a in range(blocks)]
+        for a in range(blocks):
+            nc.tensor.matmul(window[a][:], identity[:], base_tile[:, a, :], start=True, stop=False)
+
+        for a in range(blocks):
+            nc.tensor.matmul(
+                window[a][:].indirect(offsets[:]), w_tile[:, a * P : (a + 1) * P], x_tile[:], start=False, stop=True
+            )
+
+        sums = held.tile([P, blocks, V], F32)
+        for a in range(blocks):
+            t = held.tile([P, S], F32, name=f"t{a}")
+            nc.scalar.activation(
+                t[:], window[a][:], mybir.ActivationFunctionType.Tanh, bias=bias[:, a : a + 1]
+            )
+            nc.vector.tensor_reduce(
+                sums[:, a, :], t[:].rearrange("p (v d) -> p v d", d=D), mybir.AxisListType.X, mybir.AluOpType.add
+            )
+        mean = held.tile([P, blocks, V], F32)
+        nc.vector.tensor_scalar_mul(mean[:], sums[:], 1.0 / D)
+        nc.sync.dma_start(out.rearrange("(a p) v -> p a v", p=P), mean[:])

@@ -20,7 +20,7 @@ def tile_rows_unpool_mean_tanh_kernel(tc, base, x, w, b, offs, out):
         tc.psum_pool(name="windows", bufs=1) as windows,
     ):
         base_tile = held.tile([P, blocks, S], BF16)
-        nc.sync.dma_start(base_tile[:], base.rearrange("(a p) s -> p a s", p=P))
+        nc.sync.dma_start(base_tile[:], base.rearrange("(p a) s -> p a s", p=P))
         w_tile = held.tile([P, M], BF16)
         nc.sync.dma_start(w_tile[:], w.rearrange("e k m -> k (e m)"))
         x_tile = held.tile([P, N], BF16)
@@ -28,7 +28,7 @@ def tile_rows_unpool_mean_tanh_kernel(tc, base, x, w, b, offs, out):
         offsets = held.tile([P, N // 16], U16)
         nc.sync.dma_start(offsets[:], offs)
         bias = held.tile([P, blocks], F32)
-        nc.scalar.dma_start(bias[:], b.rearrange("(a p) o -> p (a o)", p=P))
+        nc.scalar.dma_start(bias[:], b.rearrange("(p a) o -> p (a o)", p=P))
 
         identity = held.tile([P, P], BF16)
         make_identity(nc, identity[:])
@@ -39,7 +39,7 @@ def tile_rows_unpool_mean_tanh_kernel(tc, base, x, w, b, offs, out):
 
         for a in range(blocks):
             nc.tensor.matmul(
-                window[a][:].indirect(offsets[:]), w_tile[:, a * P : (a + 1) * P], x_tile[:], start=False, stop=True
+                window[a][:].indirect(offsets[:]), w_tile[:, a :: blocks], x_tile[:], start=False, stop=True
             )
 
         sums = held.tile([P, blocks, V], F32)
@@ -53,4 +53,4 @@ def tile_rows_unpool_mean_tanh_kernel(tc, base, x, w, b, offs, out):
             )
         mean = held.tile([P, blocks, V], F32)
         nc.vector.tensor_scalar_mul(mean[:], sums[:], 1.0 / D)
-        nc.sync.dma_start(out.rearrange("(a p) v -> p a v", p=P), mean[:])
+        nc.sync.dma_start(out.rearrange("(p a) v -> p a v", p=P), mean[:])

@@ -4,6 +4,8 @@ from concourse.masks import make_identity
 P = 128
 D = 8
 
+WARM_UPS = 8
+
 BF16, F32, U16 = mybir.dt.bfloat16, mybir.dt.float32, mybir.dt.uint16
 FLOPS = 2 * 128 * 512 * 128
 
@@ -30,8 +32,17 @@ def tile_rows_unpool_mean_tanh_kernel(tc, base, x, w, b, offs, out):
         bias = held.tile([P, blocks], F32)
         nc.scalar.dma_start(bias[:], b.rearrange("(p a) o -> p (a o)", p=P))
 
+        zeros = held.tile([P, S], BF16)
+        nc.vector.memset(zeros[:], 0.0)
+        table_call = held.tile([P, 1], F32)
+        nc.scalar.activation(table_call[:], zeros[:, 0:1], mybir.ActivationFunctionType.Tanh)
+
         identity = held.tile([P, P], BF16)
         make_identity(nc, identity[:])
+
+        spare = windows.tile([P, S], F32)
+        for turn in range(WARM_UPS):
+            nc.tensor.matmul(spare[:], zeros[:, 0:P], zeros[:], start=True, stop=True)
 
         window = [windows.tile([P, S], F32, name=f"window{a}") for a in range(blocks)]
         for a in range(blocks):

@@ -24,7 +24,7 @@ def tile_rows_unpool_mean_tanh_kernel(tc, base, x, w, b, offs, out):
         base_tile = held.tile([P, blocks, S], BF16)
         nc.sync.dma_start(base_tile[:], base.rearrange("(p a) s -> p a s", p=P))
         w_tile = held.tile([P, M], BF16)
-        nc.sync.dma_start(w_tile[:], w.rearrange("e k m -> k (e m)"))
+        nc.scalar.dma_start(w_tile[:], w.rearrange("e k m -> k (e m)"))
         x_tile = held.tile([P, N], BF16)
         nc.sync.dma_start(x_tile[:], x)
         offsets = held.tile([P, N // 16], U16)

import concourse.mybir as mybir
from concourse.masks import make_identity

P = 128
D = 8

WARM_UPS = 8

BF16, F32, U16 = mybir.dt.bfloat16, mybir.dt.float32, mybir.dt.uint16
FLOPS = 2 * 128 * 512 * 128


def tile_rows_unpool_mean_tanh_kernel(tc, base, x, w, b, offs, out):
    nc = tc.nc
    M, S = base.shape
    N = x.shape[1]
    V = S // D
    blocks = M // P

    with (
        tc.tile_pool(name="held", bufs=1) as held,
        tc.psum_pool(name="windows", bufs=1) as windows,
    ):
        base_tile = held.tile([P, blocks, S], BF16)
        nc.sync.dma_start(base_tile[:], base.rearrange("(p a) s -> p a s", p=P))
        w_tile = held.tile([P, M], BF16)
        nc.scalar.dma_start(w_tile[:], w.rearrange("e k m -> k (e m)"))
        x_tile = held.tile([P, N], BF16)
        nc.sync.dma_start(x_tile[:], x)
        offsets = held.tile([P, N // 16], U16)
        nc.sync.dma_start(offsets[:], offs)
        bias = held.tile([P, blocks], F32)
        nc.scalar.dma_start(bias[:], b.rearrange("(p a) o -> p (a o)", p=P))

        zeros = held.tile([P, S], BF16)
        nc.vector.memset(zeros[:], 0.0)
        table_call = held.tile([P, 1], F32)
        nc.scalar.activation(table_call[:], zeros[:, 0:1], mybir.ActivationFunctionType.Tanh)

        identity = held.tile([P, P], BF16)
        make_identity(nc, identity[:])

        spare = windows.tile([P, S], F32)
        for turn in range(WARM_UPS):
            nc.tensor.matmul(spare[:], zeros[:, 0:P], zeros[:], start=True, stop=True)

        window = [windows.tile([P, S], F32, name=f"window{a}") for a in range(blocks)]
        for a in range(blocks):
            nc.tensor.matmul(window[a][:], identity[:], base_tile[:, a, :], start=True, stop=False)

        for a in range(blocks):
            nc.tensor.matmul(
                window[a][:].indirect(offsets[:]), w_tile[:, a :: blocks], x_tile[:], start=False, stop=True
            )

        sums = held.tile([P, blocks, V], F32)
        for a in range(blocks):
            t = held.tile([P, S], F32, name=f"t{a}")
            nc.scalar.activation(
                t[:], window[a][:], mybir.ActivationFunctionType.Tanh, bias=bias[:, a : a + 1]
            )
            nc.vector.tensor_reduce(
                sums[:, a, :], t[:].rearrange("p (v d) -> p v d", d=D), mybir.AxisListType.X, mybir.AluOpType.add
            )
        mean = held.tile([P, blocks, V], F32)
        nc.vector.tensor_scalar_mul(mean[:], sums[:], 1.0 / D)
        nc.sync.dma_start(out.rearrange("(p a) v -> p a v", p=P), mean[:])
